import numpy as np
import ml_dtypes


def mxq(x, axis, fmt="e4m3"):
    dtype, down = {"e4m3": (ml_dtypes.float8_e4m3fn, 7), "e5m2": (ml_dtypes.float8_e5m2, 14)}[fmt]
    v = np.moveaxis(np.asarray(x, np.float32).astype(ml_dtypes.bfloat16).astype(np.float64), axis, -1)
    blocks = v.reshape(v.shape[:-1] + (-1, 32))
    amax = np.abs(blocks).max(-1, keepdims=True)
    byte = np.maximum(np.where(amax > 0, np.frexp(amax)[1] - 1 + 127, 0) - down, 1)
    scale = np.exp2(byte - 127.0)
    codes = (blocks / scale).astype(np.float32).astype(dtype).astype(np.float64)
    return np.moveaxis((codes * scale).reshape(v.shape), -1, axis)


WIDE = False


def mx_kscale(k):
    if not WIDE:
        return np.ones(k)
    levels = np.array([10, -10, 5, -5, 0])
    if k % 512:
        return np.exp2(np.random.permutation(np.resize(levels, k // 32))).repeat(32)
    a = np.empty((k // 512, 16))
    for p in range(k // 512):
        a[p, :8] = np.random.permutation(np.resize(levels, 8))
        for g in range(8):
            far = levels[np.abs(levels - a[p, g]) >= 10]
            a[p, g + 8] = far[np.random.randint(len(far))]
    return np.exp2(a.ravel()).repeat(32)


def f64(x):
    return np.asarray(x).astype(np.float64)


def striped8(idx):
    return np.asarray(idx).reshape(8, -1, 16).transpose(0, 2, 1).reshape(128, -1).astype(np.uint16)


def unstriped8(offs):
    return offs.reshape(8, 16, -1).transpose(0, 2, 1).reshape(8, -1).astype(np.int64)


def pick8(x, idx, run):
    r = np.arange(len(x))
    return x[r[:, None], idx[r % (8 * run) // run]]


E2M1 = np.array([0.0, 0.5, 1.0, 1.5, 2.0, 3.0, 4.0, 6.0, -0.0, -0.5, -1.0, -1.5, -2.0, -3.0, -4.0, -6.0])


def pack_weight(w, fmt):
    k, n = w.shape
    w = f64(np.asarray(w, np.float32).astype(ml_dtypes.bfloat16)).reshape(k // 32, 32, n)
    amax = np.abs(w).max(1)
    if fmt == "e4m3":
        byte = np.frexp(amax)[1] - 1 + 127 - 7
    else:
        mant, ex = np.frexp(amax / 6.0)
        byte = np.where(mant > 0.5, ex, ex - 1) + 127
    byte = np.clip(np.where(amax > 0, byte, 1), 1, 254)
    scaled = (w * np.exp2(127.0 - byte)[:, None, :]).reshape(k, n).astype(np.float32)
    by_word = np.ascontiguousarray(scaled.reshape(k // 512, 128, 4, n).transpose(0, 1, 3, 2))
    if fmt == "e4m3":
        words = by_word.astype(ml_dtypes.float8_e4m3fn).view(np.uint8)
    else:
        c = by_word.astype(ml_dtypes.float4_e2m1fn).view(np.uint8) & 0xF
        words = (c[..., 0::2] | (c[..., 1::2] << 4)).reshape(k // 512, 128, 2 * n)
    return np.ascontiguousarray(words), np.ascontiguousarray(byte.astype(np.uint8).reshape(k // 512, 16, n))


def unpack_weight(words, scales, fmt):
    g, _, n = scales.shape
    words = np.ascontiguousarray(words).reshape(g, 128, n, -1)
    if fmt == "e4m3":
        vals = words.view(ml_dtypes.float8_e4m3fn).astype(np.float64)
    else:
        nib = np.empty((g, 128, n, 4), np.uint8)
        nib[..., 0::2] = words & 0xF
        nib[..., 1::2] = words >> 4
        vals = E2M1[nib]
    vals = vals * np.repeat(np.exp2(scales.astype(np.float64) - 127.0), 8, axis=1)[..., None]
    return vals.transpose(0, 1, 3, 2).reshape(g * 512, n)


def sigmoid(v):
    return 1.0 / (1.0 + np.exp(-v))


D, E, T, Q, I = 512, 512, 1024, 128, 512


def setup_inputs():
    n = np.random.standard_normal
    idx = np.stack([np.random.permutation(T)[:I] for _ in range(8)])
    fd = mx_kscale(D)
    fe = mx_kscale(E)
    keysp = pack_weight(n((D, T)) / fd[:, None], "e4m3")
    return {
        "query": (n((D, Q)) * 0.5 / np.sqrt(D) * fd[:, None]).astype(np.float32),
        "keys_words": keysp[0],
        "keys_scales": keysp[1],
        "gout": (n((E, Q)) * 1 / np.sqrt(E) * fe[:, None]).astype(np.float32),
        "vals": (n((E, T)) / fe[:, None]).astype(np.float32),
        "lse": (np.random.uniform(6.8, 7.2, (Q, 1))).astype(np.float32),
        "delta": (np.random.uniform(-0.3, 0.3, (Q, 1))).astype(np.float32),
        "steep": (np.random.uniform(2.0, 6.0, (Q, 1))).astype(np.float32),
        "old": (0.5 * n((Q, I))).astype(np.float32),
        "offs": striped8(idx),
    }


def reference(query, keys_words, keys_scales, gout, vals, lse, delta, steep, old, offs):
    idx = unstriped8(offs)
    keysu = unpack_weight(keys_words, keys_scales, "e4m3")
    queryq = mxq(f64(query), 0, "e4m3")
    a = queryq.T @ keysu
    goutq = mxq(f64(gout), 0, "e4m3")
    valsq = mxq(f64(vals), 0, "e4m3")
    dp = goutq.T @ valsq
    ds = np.exp(a - f64(lse)) * (dp - f64(delta)) * 1024.0
    y = pick8(ds, idx, 16) * sigmoid(pick8(a, idx, 16) * f64(steep)) + f64(old)
    return y

@@ -1,0 +1,152 @@
+import math
+from contextlib import ExitStack
+
+import concourse.mybir as mybir
+
+D, E, T, Q, SLOTS = 512, 512, 1024, 128, 512
+FLOPS = 2 * Q * T * (D + E)
+
+F32 = mybir.dt.float32
+BF16 = mybir.dt.bfloat16
+I32 = mybir.dt.int32
+U32 = mybir.dt.uint32
+U16 = mybir.dt.uint16
+U8 = mybir.dt.uint8
+FP8X4 = mybir.dt.float8_e4m3fn_x4
+ALU = mybir.AluOpType
+ACT = mybir.ActivationFunctionType
+
+P = 128
+PACK = 4
+BANK = 512
+
+LOADS = (
+    (0, 512, ((0, 256, "vector"), (256, 256, "scalar"))),
+    (512, 384, ((512, 256, "vector"), (768, 128, "scalar"))),
+    (896, 128, ((896, 128, "scalar"),)),
+)
+
+
+def interleave(nc, engine, grouped, raw):
+    out = grouped.rearrange("p (c i) t -> p c t i", i=4)
+    src = raw.rearrange("p t (c i) -> p c t i", i=4)
+    if engine == "vector":
+        nc.vector.tensor_copy(out=out, in_=src)
+    else:
+        nc.scalar.copy(out=out, in_=src)
+
+
+def quantize(nc, pool, name, grouped, width):
+    codes = pool.tile([P, width], U32, name=name + "_codes", align_bytes=64)
+    scales = pool.tile([P, width], U8, name=name + "_scales", align_bytes=64)
+    nc.vector.quantize_mx(out=codes[:].bitcast(FP8X4), scales=scales[:], in_=grouped.rearrange("p w t -> p (w t)"))
+    return codes, scales
+
+
+def tile_attend_gboost_heads_kernel(tc, query, keys_words, keys_scales, gout, vals, lse, delta, steep, old, offs, out):
+    nc = tc.nc
+    with ExitStack() as ctx:
+        keep = ctx.enter_context(tc.tile_pool(name="keep", bufs=1))
+        psum = ctx.enter_context(tc.psum_pool(name="psum", bufs=1))
+
+        offsets = keep.tile([P, SLOTS // 16], U16, name="offsets")
+        q_raw = keep.tile([P, PACK, Q], F32, name="q_raw")
+        g_raw = keep.tile([P, PACK, Q], F32, name="g_raw")
+        k_codes = keep.tile([P, T], U32, name="k_codes", align_bytes=64)
+        k_scales = keep.tile([P, T], U8, name="k_scales", align_bytes=64)
+        lse_sb = keep.tile([P, 1], F32, name="lse_sb")
+        delta_sb = keep.tile([P, 1], F32, name="delta_sb")
+        steep_sb = keep.tile([P, 1], F32, name="steep_sb")
+        old_sb = keep.tile([P, SLOTS], F32, name="old_sb")
+
+        warm_in = keep.tile([P, 1], F32, name="warm_in")
+        warm_out = keep.tile([P, 1], F32, name="warm_out")
+        nc.vector.memset(warm_in[:], 0.0)
+
+        nc.sync.dma_start(out=q_raw[:], in_=query.rearrange("(p j) w -> p j w", j=PACK))
+        for quad in range(4):
+            nc.scalar.dma_start(
+                out=k_scales[32 * quad : 32 * quad + 4, :].bitcast(I32),
+                in_=keys_scales[0, 4 * quad : 4 * quad + 4, :].bitcast(I32),
+            )
+        nc.sync.dma_start(out=k_codes[:].bitcast(I32), in_=keys_words[0].rearrange("p n t -> p (n t)").bitcast(I32))
+        nc.sync.dma_start(out=g_raw[:], in_=gout.rearrange("(p j) w -> p j w", j=PACK))
+        nc.scalar.dma_start(out=lse_sb[:], in_=lse)
+        nc.scalar.activation(out=warm_out[:], in_=warm_in[:], func=ACT.Exp)
+        nc.sync.dma_start(offsets[:], offs)
+        nc.scalar.dma_start(out=steep_sb[:], in_=steep)
+        nc.scalar.dma_start(out=delta_sb[:], in_=delta)
+        v_rows = vals.rearrange("(p j) w -> p j w", j=PACK)
+        v_raw = []
+        for n, (first, width, pieces) in enumerate(LOADS):
+            raw = keep.tile([P, PACK, width], F32, name=f"v_raw{n}")
+            nc.sync.dma_start(out=raw[:], in_=v_rows[:, :, first : first + width])
+            v_raw.append(raw)
+        nc.sync.dma_start(out=old_sb[:], in_=old)
+
+        q_grp = keep.tile([P, Q, PACK], BF16, name="q_grp", align_bytes=64)
+        g_grp = keep.tile([P, Q, PACK], BF16, name="g_grp", align_bytes=64)
+        interleave(nc, "vector", q_grp[:], q_raw[:])
+        q_codes, q_scales = quantize(nc, keep, "q", q_grp[:], Q)
+        interleave(nc, "vector", g_grp[:], g_raw[:])
+        g_codes, g_scales = quantize(nc, keep, "g", g_grp[:], Q)
+
+        exp_bias = keep.tile([P, 1], F32, name="exp_bias")
+        half_steep = keep.tile([P, 1], F32, name="half_steep")
+        nc.vector.tensor_scalar(out=exp_bias[:], in0=lse_sb[:], scalar1=-1.0, scalar2=math.log(1024.0), op0=ALU.mult, op1=ALU.add)
+        nc.vector.tensor_scalar(out=half_steep[:], in0=steep_sb[:], scalar1=0.5, scalar2=None, op0=ALU.mult)
+
+        a_sb = keep.tile([P, T], F32, name="a_sb")
+        for h in range(T // BANK):
+            cols = slice(h * BANK, (h + 1) * BANK)
+            a_ps = psum.tile([P, BANK], F32, name=f"a_ps{h}")
+            nc.tensor.matmul_mx(
+                out=a_ps[:], lhsT=q_codes[:].bitcast(FP8X4), lhsT_scale=q_scales[:],
+                rhs=k_codes[:, cols].bitcast(FP8X4), rhs_scale=k_scales[:, cols], start=True, stop=True,
+            )
+            if h == 0:
+                nc.scalar.copy(out=a_sb[:, cols], in_=a_ps[:])
+            else:
+                nc.vector.tensor_copy(out=a_sb[:, cols], in_=a_ps[:])
+
+        weight = keep.tile([P, T], F32, name="weight")
+        nc.scalar.activation(out=weight[:], in_=a_sb[:], func=ACT.Exp, bias=exp_bias[:])
+        a_picked = keep.tile([P, SLOTS], F32, name="a_picked")
+        nc.vector.tensor_copy(a_picked[:], a_sb[:].indirect(offsets[:]))
+        th = keep.tile([P, SLOTS], F32, name="th")
+        nc.scalar.activation(out=th[:], in_=a_picked[:], func=ACT.Tanh, scale=half_steep[:])
+        gate = keep.tile([P, SLOTS], F32, name="gate")
+        nc.vector.tensor_scalar(out=gate[:], in0=th[:], scalar1=0.5, scalar2=0.5, op0=ALU.mult, op1=ALU.add)
+
+        ds = keep.tile([P, T], F32, name="ds")
+        for raw, (first, width, pieces) in zip(v_raw, LOADS):
+            grouped = []
+            for start, count, engine in pieces:
+                grp = keep.tile([P, count, PACK], BF16, name=f"v_grp{start}", align_bytes=64)
+                interleave(nc, engine, grp[:], raw[:, :, start - first : start - first + count])
+                grouped.append(grp)
+            for grp, (start, count, engine) in zip(grouped, pieces):
+                v_codes, v_scales = quantize(nc, keep, f"v{start}", grp[:], count)
+                dp = psum.tile([P, count], F32, name=f"dp{start}")
+                nc.tensor.matmul_mx(
+                    out=dp[:], lhsT=g_codes[:].bitcast(FP8X4), lhsT_scale=g_scales[:],
+                    rhs=v_codes[:].bitcast(FP8X4), rhs_scale=v_scales[:], start=True, stop=True,
+                )
+                cols = slice(start, start + count)
+                nc.vector.scalar_tensor_tensor(
+                    out=ds[:, cols], in0=dp[:], scalar=delta_sb[:], in1=weight[:, cols], op0=ALU.subtract, op1=ALU.mult
+                )
+
+        halves = 2
+        width = SLOTS // halves
+        gated = keep.tile([P, SLOTS], F32, name="gated")
+        for h in range(halves):
+            cols = slice(h * width, (h + 1) * width)
+            nc.vector.tensor_tensor(
+                gated[:, cols], ds[:].indirect(offsets[:, h * width // 16 : (h + 1) * width // 16]), gate[:, cols], ALU.mult
+            )
+        for h in range(halves):
+            cols = slice(h * width, (h + 1) * width)
+            res = keep.tile([P, width], F32, name=f"res{h}")
+            nc.vector.tensor_tensor(res[:], gated[:, cols], old_sb[:, cols], ALU.add)
+            nc.sync.dma_start(out=out[:, cols], in_=res[:])

@@ -19,10 +19,11 @@ ACT = mybir.ActivationFunctionType
 P = 128
 PACK = 4
 BANK = 512
+A_WIDTH = 256
 
 LOADS = (
     (0, 512, ((0, 256, "vector"), (256, 256, "scalar"))),
-    (512, 384, ((512, 256, "vector"), (768, 128, "scalar"))),
+    (512, 384, ((512, 128, "scalar"), (640, 256, "vector"))),
     (896, 128, ((896, 128, "scalar"),)),
 )
 
@@ -53,89 +54,96 @@ def tile_attend_gboost_heads_kernel(tc, query, keys_words, keys_scales, gout, va
         q_raw = keep.tile([P, PACK, Q], F32, name="q_raw")
         g_raw = keep.tile([P, PACK, Q], F32, name="g_raw")
         k_codes = keep.tile([P, T], U32, name="k_codes", align_bytes=64)
-        k_scales = keep.tile([P, T], U8, name="k_scales", align_bytes=64)
-        lse_sb = keep.tile([P, 1], F32, name="lse_sb")
-        delta_sb = keep.tile([P, 1], F32, name="delta_sb")
-        steep_sb = keep.tile([P, 1], F32, name="steep_sb")
+        k_scales = keep.tile([P, A_WIDTH], U8, name="k_scales", align_bytes=64)
+        lse_t = keep.tile([P, 1], F32, name="lse_t")
+        steep_t = keep.tile([P, 1], F32, name="steep_t")
+        delta_t = keep.tile([P, 1], F32, name="delta_t")
+        lse_sb, steep_sb, delta_sb = lse_t[:], steep_t[:], delta_t[:]
+        warm_out = keep.tile([P, 1], F32, name="warm_out")
         old_sb = keep.tile([P, SLOTS], F32, name="old_sb")
 
         warm_in = keep.tile([P, 1], F32, name="warm_in")
-        warm_out = keep.tile([P, 1], F32, name="warm_out")
         nc.vector.memset(warm_in[:], 0.0)
+        nc.scalar.activation(out=warm_out[:], in_=warm_in[:], func=ACT.Exp)
 
+        nc.sync.dma_start(offsets[:], offs)
         nc.sync.dma_start(out=q_raw[:], in_=query.rearrange("(p j) w -> p j w", j=PACK))
         for quad in range(4):
-            nc.scalar.dma_start(
-                out=k_scales[32 * quad : 32 * quad + 4, :].bitcast(I32),
-                in_=keys_scales[0, 4 * quad : 4 * quad + 4, :].bitcast(I32),
+            nc.sync.dma_start(
+                out=k_scales[32 * quad : 32 * quad + 16, :].bitcast(I32),
+                in_=keys_scales[0, 4 * quad : 4 * quad + 4, :].bitcast(I32).rearrange("f (h c) -> h f c", h=T // A_WIDTH),
             )
         nc.sync.dma_start(out=k_codes[:].bitcast(I32), in_=keys_words[0].rearrange("p n t -> p (n t)").bitcast(I32))
         nc.sync.dma_start(out=g_raw[:], in_=gout.rearrange("(p j) w -> p j w", j=PACK))
-        nc.scalar.dma_start(out=lse_sb[:], in_=lse)
-        nc.scalar.activation(out=warm_out[:], in_=warm_in[:], func=ACT.Exp)
-        nc.sync.dma_start(offsets[:], offs)
-        nc.scalar.dma_start(out=steep_sb[:], in_=steep)
-        nc.scalar.dma_start(out=delta_sb[:], in_=delta)
+        nc.sync.dma_start(out=lse_sb, in_=lse)
         v_rows = vals.rearrange("(p j) w -> p j w", j=PACK)
         v_raw = []
         for n, (first, width, pieces) in enumerate(LOADS):
-            raw = keep.tile([P, PACK, width], F32, name=f"v_raw{n}")
+            raw = keep.tile([P, PACK, width], F32, name=f"v_raw{n}", tag=f"v_raw{n}")
             nc.sync.dma_start(out=raw[:], in_=v_rows[:, :, first : first + width])
             v_raw.append(raw)
+            if n == 0:
+                nc.sync.dma_start(out=steep_sb, in_=steep)
+                nc.sync.dma_start(out=delta_sb, in_=delta)
         nc.sync.dma_start(out=old_sb[:], in_=old)
 
         q_grp = keep.tile([P, Q, PACK], BF16, name="q_grp", align_bytes=64)
         g_grp = keep.tile([P, Q, PACK], BF16, name="g_grp", align_bytes=64)
         interleave(nc, "vector", q_grp[:], q_raw[:])
         q_codes, q_scales = quantize(nc, keep, "q", q_grp[:], Q)
-        interleave(nc, "vector", g_grp[:], g_raw[:])
-        g_codes, g_scales = quantize(nc, keep, "g", g_grp[:], Q)
+        interleave(nc, "scalar", g_grp[:], g_raw[:])
 
         exp_bias = keep.tile([P, 1], F32, name="exp_bias")
         half_steep = keep.tile([P, 1], F32, name="half_steep")
-        nc.vector.tensor_scalar(out=exp_bias[:], in0=lse_sb[:], scalar1=-1.0, scalar2=math.log(1024.0), op0=ALU.mult, op1=ALU.add)
-        nc.vector.tensor_scalar(out=half_steep[:], in0=steep_sb[:], scalar1=0.5, scalar2=None, op0=ALU.mult)
+        nc.gpsimd.tensor_scalar(out=exp_bias[:], in0=lse_sb, scalar1=-1.0, scalar2=math.log(1024.0), op0=ALU.mult, op1=ALU.add)
+        nc.gpsimd.tensor_scalar(out=half_steep[:], in0=steep_sb, scalar1=0.5, scalar2=0.0, op0=ALU.mult, op1=ALU.add)
 
         a_sb = keep.tile([P, T], F32, name="a_sb")
-        for h in range(T // BANK):
-            cols = slice(h * BANK, (h + 1) * BANK)
-            a_ps = psum.tile([P, BANK], F32, name=f"a_ps{h}")
+        weight = keep.tile([P, T], F32, name="weight")
+        for h in range(T // A_WIDTH):
+            cols = slice(h * A_WIDTH, (h + 1) * A_WIDTH)
+            a_ps = psum.tile([P, A_WIDTH], F32, name=f"a_ps{h}", tag=f"bank{h}")
             nc.tensor.matmul_mx(
                 out=a_ps[:], lhsT=q_codes[:].bitcast(FP8X4), lhsT_scale=q_scales[:],
-                rhs=k_codes[:, cols].bitcast(FP8X4), rhs_scale=k_scales[:, cols], start=True, stop=True,
+                rhs=k_codes[:, cols].bitcast(FP8X4), rhs_scale=k_scales[4 * h : P, :], start=True, stop=True,
             )
-            if h == 0:
-                nc.scalar.copy(out=a_sb[:, cols], in_=a_ps[:])
-            else:
-                nc.vector.tensor_copy(out=a_sb[:, cols], in_=a_ps[:])
-
-        weight = keep.tile([P, T], F32, name="weight")
-        nc.scalar.activation(out=weight[:], in_=a_sb[:], func=ACT.Exp, bias=exp_bias[:])
+            nc.vector.tensor_copy(out=a_sb[:, cols], in_=a_ps[:])
+        for h in range(T // BANK):
+            cols = slice(h * BANK, (h + 1) * BANK)
+            nc.scalar.activation(out=weight[:, cols], in_=a_sb[:, cols], func=ACT.Exp, bias=exp_bias[:])
+        g_codes, g_scales = quantize(nc, keep, "g", g_grp[:], Q)
         a_picked = keep.tile([P, SLOTS], F32, name="a_picked")
         nc.vector.tensor_copy(a_picked[:], a_sb[:].indirect(offsets[:]))
-        th = keep.tile([P, SLOTS], F32, name="th")
-        nc.scalar.activation(out=th[:], in_=a_picked[:], func=ACT.Tanh, scale=half_steep[:])
-        gate = keep.tile([P, SLOTS], F32, name="gate")
-        nc.vector.tensor_scalar(out=gate[:], in0=th[:], scalar1=0.5, scalar2=0.5, op0=ALU.mult, op1=ALU.add)
 
         ds = keep.tile([P, T], F32, name="ds")
-        for raw, (first, width, pieces) in zip(v_raw, LOADS):
+        th = keep.tile([P, SLOTS], F32, name="th")
+        bank = T // A_WIDTH
+        for n, (raw, (first, width, pieces)) in enumerate(zip(v_raw, LOADS)):
             grouped = []
             for start, count, engine in pieces:
                 grp = keep.tile([P, count, PACK], BF16, name=f"v_grp{start}", align_bytes=64)
                 interleave(nc, engine, grp[:], raw[:, :, start - first : start - first + count])
                 grouped.append(grp)
+            if n == 0:
+                nc.scalar.activation(out=th[:], in_=a_picked[:], func=ACT.Tanh, scale=half_steep[:])
+            products = []
             for grp, (start, count, engine) in zip(grouped, pieces):
                 v_codes, v_scales = quantize(nc, keep, f"v{start}", grp[:], count)
-                dp = psum.tile([P, count], F32, name=f"dp{start}")
+                dp = psum.tile([P, count], F32, name=f"dp{start}", tag=f"bank{bank % 8}")
+                bank += 1
                 nc.tensor.matmul_mx(
                     out=dp[:], lhsT=g_codes[:].bitcast(FP8X4), lhsT_scale=g_scales[:],
                     rhs=v_codes[:].bitcast(FP8X4), rhs_scale=v_scales[:], start=True, stop=True,
                 )
+                products.append(dp)
+            for dp, (start, count, engine) in zip(products, pieces):
                 cols = slice(start, start + count)
                 nc.vector.scalar_tensor_tensor(
-                    out=ds[:, cols], in0=dp[:], scalar=delta_sb[:], in1=weight[:, cols], op0=ALU.subtract, op1=ALU.mult
+                    out=ds[:, cols], in0=dp[:], scalar=delta_sb, in1=weight[:, cols], op0=ALU.subtract, op1=ALU.mult
                 )
+
+        gate = keep.tile([P, SLOTS], F32, name="gate", tag=f"v_raw{len(LOADS) - 1}")
+        nc.scalar.activation(out=gate[:], in_=th[:], func=ACT.Copy, scale=0.5, bias=0.5)
 
         halves = 2
         width = SLOTS // halves

@@ -22,9 +22,10 @@ BANK = 512
 A_WIDTH = 256
 
 LOADS = (
-    (0, 512, ((0, 256, "vector"), (256, 256, "scalar"))),
-    (512, 384, ((512, 128, "scalar"), (640, 256, "vector"))),
-    (896, 128, ((896, 128, "scalar"),)),
+    (0, 256, 0),
+    (256, 256, 128),
+    (512, 256, 128),
+    (768, 256, 128),
 )
 
 
@@ -66,7 +67,16 @@ def tile_attend_gboost_heads_kernel(tc, query, keys_words, keys_scales, gout, va
         nc.vector.memset(warm_in[:], 0.0)
         nc.scalar.activation(out=warm_out[:], in_=warm_in[:], func=ACT.Exp)
 
-        nc.sync.dma_start(offsets[:], offs)
+        v_rows = vals.rearrange("(p j) w -> p j w", j=PACK)
+        v_raw = []
+
+        def load_vals(n):
+            first, width, on_vector = LOADS[n]
+            raw = keep.tile([P, PACK, width], F32, name=f"v_raw{n}", tag=f"v_raw{n}")
+            nc.sync.dma_start(out=raw[:], in_=v_rows[:, :, first : first + width])
+            v_raw.append(raw)
+
+        nc.sync.dma_start(out=lse_sb, in_=lse)
         nc.sync.dma_start(out=q_raw[:], in_=query.rearrange("(p j) w -> p j w", j=PACK))
         for quad in range(4):
             nc.sync.dma_start(
@@ -74,24 +84,20 @@ def tile_attend_gboost_heads_kernel(tc, query, keys_words, keys_scales, gout, va
                 in_=keys_scales[0, 4 * quad : 4 * quad + 4, :].bitcast(I32).rearrange("f (h c) -> h f c", h=T // A_WIDTH),
             )
         nc.sync.dma_start(out=k_codes[:].bitcast(I32), in_=keys_words[0].rearrange("p n t -> p (n t)").bitcast(I32))
+        load_vals(0)
         nc.sync.dma_start(out=g_raw[:], in_=gout.rearrange("(p j) w -> p j w", j=PACK))
-        nc.sync.dma_start(out=lse_sb, in_=lse)
-        v_rows = vals.rearrange("(p j) w -> p j w", j=PACK)
-        v_raw = []
-        for n, (first, width, pieces) in enumerate(LOADS):
-            raw = keep.tile([P, PACK, width], F32, name=f"v_raw{n}", tag=f"v_raw{n}")
-            nc.sync.dma_start(out=raw[:], in_=v_rows[:, :, first : first + width])
-            v_raw.append(raw)
-            if n == 0:
-                nc.sync.dma_start(out=steep_sb, in_=steep)
-                nc.sync.dma_start(out=delta_sb, in_=delta)
+        nc.sync.dma_start(offsets[:], offs)
+        nc.sync.dma_start(out=delta_sb, in_=delta)
+        load_vals(1)
+        nc.sync.dma_start(out=steep_sb, in_=steep)
+        for n in range(2, len(LOADS)):
+            load_vals(n)
         nc.sync.dma_start(out=old_sb[:], in_=old)
 
         q_grp = keep.tile([P, Q, PACK], BF16, name="q_grp", align_bytes=64)
         g_grp = keep.tile([P, Q, PACK], BF16, name="g_grp", align_bytes=64)
         interleave(nc, "vector", q_grp[:], q_raw[:])
         q_codes, q_scales = quantize(nc, keep, "q", q_grp[:], Q)
-        interleave(nc, "scalar", g_grp[:], g_raw[:])
 
         exp_bias = keep.tile([P, 1], F32, name="exp_bias")
         half_steep = keep.tile([P, 1], F32, name="half_steep")
@@ -99,7 +105,6 @@ def tile_attend_gboost_heads_kernel(tc, query, keys_words, keys_scales, gout, va
         nc.gpsimd.tensor_scalar(out=half_steep[:], in0=steep_sb, scalar1=0.5, scalar2=0.0, op0=ALU.mult, op1=ALU.add)
 
         a_sb = keep.tile([P, T], F32, name="a_sb")
-        weight = keep.tile([P, T], F32, name="weight")
         for h in range(T // A_WIDTH):
             cols = slice(h * A_WIDTH, (h + 1) * A_WIDTH)
             a_ps = psum.tile([P, A_WIDTH], F32, name=f"a_ps{h}", tag=f"bank{h}")
@@ -108,41 +113,58 @@ def tile_attend_gboost_heads_kernel(tc, query, keys_words, keys_scales, gout, va
                 rhs=k_codes[:, cols].bitcast(FP8X4), rhs_scale=k_scales[4 * h : P, :], start=True, stop=True,
             )
             nc.vector.tensor_copy(out=a_sb[:, cols], in_=a_ps[:])
-        for h in range(T // BANK):
-            cols = slice(h * BANK, (h + 1) * BANK)
-            nc.scalar.activation(out=weight[:, cols], in_=a_sb[:, cols], func=ACT.Exp, bias=exp_bias[:])
+        interleave(nc, "vector", g_grp[:], g_raw[:])
         g_codes, g_scales = quantize(nc, keep, "g", g_grp[:], Q)
         a_picked = keep.tile([P, SLOTS], F32, name="a_picked")
         nc.vector.tensor_copy(a_picked[:], a_sb[:].indirect(offsets[:]))
 
         ds = keep.tile([P, T], F32, name="ds")
         th = keep.tile([P, SLOTS], F32, name="th")
-        bank = T // A_WIDTH
-        for n, (raw, (first, width, pieces)) in enumerate(zip(v_raw, LOADS)):
-            grouped = []
-            for start, count, engine in pieces:
-                grp = keep.tile([P, count, PACK], BF16, name=f"v_grp{start}", align_bytes=64)
-                interleave(nc, engine, grp[:], raw[:, :, start - first : start - first + count])
-                grouped.append(grp)
-            if n == 0:
-                nc.scalar.activation(out=th[:], in_=a_picked[:], func=ACT.Tanh, scale=half_steep[:])
-            products = []
-            for grp, (start, count, engine) in zip(grouped, pieces):
-                v_codes, v_scales = quantize(nc, keep, f"v{start}", grp[:], count)
-                dp = psum.tile([P, count], F32, name=f"dp{start}", tag=f"bank{bank % 8}")
-                bank += 1
-                nc.tensor.matmul_mx(
-                    out=dp[:], lhsT=g_codes[:].bitcast(FP8X4), lhsT_scale=g_scales[:],
-                    rhs=v_codes[:].bitcast(FP8X4), rhs_scale=v_scales[:], start=True, stop=True,
-                )
-                products.append(dp)
-            for dp, (start, count, engine) in zip(products, pieces):
-                cols = slice(start, start + count)
-                nc.vector.scalar_tensor_tensor(
-                    out=ds[:, cols], in0=dp[:], scalar=delta_sb, in1=weight[:, cols], op0=ALU.subtract, op1=ALU.mult
-                )
 
-        gate = keep.tile([P, SLOTS], F32, name="gate", tag=f"v_raw{len(LOADS) - 1}")
+        def quantize_load(n):
+            first, width, on_vector = LOADS[n]
+            parts = []
+            for engine, lo, hi in (("vector", 0, on_vector), ("scalar", on_vector, width)):
+                if hi > lo:
+                    grp = keep.tile([P, hi - lo, PACK], BF16, name=f"v_grp{n}_{engine}", tag=f"v_grp{n}_{engine}", align_bytes=64)
+                    interleave(nc, engine, grp[:], v_raw[n][:, :, lo:hi])
+                    parts.append((grp, lo, hi))
+            v_codes = keep.tile([P, width], U32, name=f"v_codes{n}", align_bytes=64)
+            v_scales = keep.tile([P, width], U8, name=f"v_scales{n}", align_bytes=64)
+            for grp, lo, hi in reversed(parts):
+                nc.vector.quantize_mx(
+                    out=v_codes[:, lo:hi].bitcast(FP8X4), scales=v_scales[:, lo:hi], in_=grp[:].rearrange("p w t -> p (w t)")
+                )
+            return v_codes, v_scales
+
+        def multiply(dp, operand):
+            v_codes, v_scales = operand
+            nc.tensor.matmul_mx(
+                out=dp, lhsT=g_codes[:].bitcast(FP8X4), lhsT_scale=g_scales[:],
+                rhs=v_codes[:].bitcast(FP8X4), rhs_scale=v_scales[:], start=True, stop=True,
+            )
+
+        def gradient(dp, first, width, tag):
+            cols = slice(first, first + width)
+            weight = keep.tile([P, width], F32, name=f"weight{first}", tag=tag)
+            nc.scalar.activation(out=weight[:], in_=a_sb[:, cols], func=ACT.Exp, bias=exp_bias[:])
+            nc.vector.scalar_tensor_tensor(
+                out=ds[:, cols], in0=dp[:], scalar=delta_sb, in1=weight[:], op0=ALU.subtract, op1=ALU.mult
+            )
+
+        last = len(LOADS) - 1
+        products = []
+        for n, (first, width, on_vector) in enumerate(LOADS):
+            dp = psum.tile([P, width], F32, name=f"dp{n}")
+            multiply(dp[:], quantize_load(n))
+            products.append(dp)
+            if n == 1:
+                nc.scalar.activation(out=th[:], in_=a_picked[:], func=ACT.Tanh, scale=half_steep[:])
+            if n > 0:
+                gradient(products[n - 1], LOADS[n - 1][0], LOADS[n - 1][1], f"v_raw{n}")
+        gradient(products[last], LOADS[last][0], LOADS[last][1], "weight_last")
+
+        gate = keep.tile([P, SLOTS], F32, name="gate", tag=f"v_grp{last}_scalar", align_bytes=64)
         nc.scalar.activation(out=gate[:], in_=th[:], func=ACT.Copy, scale=0.5, bias=0.5)
 
         halves = 2

@@ -23,9 +23,9 @@ A_WIDTH = 256
 
 LOADS = (
     (0, 256, 0),
-    (256, 256, 128),
-    (512, 256, 128),
-    (768, 256, 128),
+    (256, 256, 192),
+    (512, 256, 160),
+    (768, 256, 160),
 )
 
 
@@ -54,7 +54,6 @@ def tile_attend_gboost_heads_kernel(tc, query, keys_words, keys_scales, gout, va
         offsets = keep.tile([P, SLOTS // 16], U16, name="offsets")
         q_raw = keep.tile([P, PACK, Q], F32, name="q_raw")
         g_raw = keep.tile([P, PACK, Q], F32, name="g_raw")
-        k_codes = keep.tile([P, T], U32, name="k_codes", align_bytes=64)
         k_scales = keep.tile([P, A_WIDTH], U8, name="k_scales", align_bytes=64)
         lse_t = keep.tile([P, 1], F32, name="lse_t")
         steep_t = keep.tile([P, 1], F32, name="steep_t")
@@ -69,28 +68,35 @@ def tile_attend_gboost_heads_kernel(tc, query, keys_words, keys_scales, gout, va
 
         v_rows = vals.rearrange("(p j) w -> p j w", j=PACK)
         v_raw = []
+        reused = []
 
         def load_vals(n):
             first, width, on_vector = LOADS[n]
-            raw = keep.tile([P, PACK, width], F32, name=f"v_raw{n}", tag=f"v_raw{n}")
-            nc.sync.dma_start(out=raw[:], in_=v_rows[:, :, first : first + width])
+            landing = keep.tile([P, PACK * width + 512], F32, name=f"landing{n}")
+            raw = landing[:, 0 : PACK * width].rearrange("p (j w) -> p j w", j=PACK)
+            nc.sync.dma_start(out=raw, in_=v_rows[:, :, first : first + width])
             v_raw.append(raw)
+            reused.append(landing[:, (PACK - 1) * width + on_vector : PACK * width + 512])
 
-        nc.sync.dma_start(out=lse_sb, in_=lse)
         nc.sync.dma_start(out=q_raw[:], in_=query.rearrange("(p j) w -> p j w", j=PACK))
         for quad in range(4):
             nc.sync.dma_start(
                 out=k_scales[32 * quad : 32 * quad + 16, :].bitcast(I32),
                 in_=keys_scales[0, 4 * quad : 4 * quad + 4, :].bitcast(I32).rearrange("f (h c) -> h f c", h=T // A_WIDTH),
             )
-        nc.sync.dma_start(out=k_codes[:].bitcast(I32), in_=keys_words[0].rearrange("p n t -> p (n t)").bitcast(I32))
+        k_words = keys_words[0].rearrange("p n t -> p (n t)").bitcast(I32)
+        k_codes = []
+        for h in range(T // BANK):
+            half = keep.tile([P, BANK], U32, name=f"k_codes{h}", align_bytes=64)
+            nc.sync.dma_start(out=half[:].bitcast(I32), in_=k_words[:, h * BANK : (h + 1) * BANK])
+            k_codes.append(half)
         load_vals(0)
-        nc.sync.dma_start(out=g_raw[:], in_=gout.rearrange("(p j) w -> p j w", j=PACK))
         nc.sync.dma_start(offsets[:], offs)
-        nc.sync.dma_start(out=delta_sb, in_=delta)
-        load_vals(1)
+        nc.sync.dma_start(out=g_raw[:], in_=gout.rearrange("(p j) w -> p j w", j=PACK))
         nc.sync.dma_start(out=steep_sb, in_=steep)
-        for n in range(2, len(LOADS)):
+        nc.sync.dma_start(out=lse_sb, in_=lse)
+        nc.sync.dma_start(out=delta_sb, in_=delta)
+        for n in range(1, len(LOADS)):
             load_vals(n)
         nc.sync.dma_start(out=old_sb[:], in_=old)
 
@@ -101,8 +107,8 @@ def tile_attend_gboost_heads_kernel(tc, query, keys_words, keys_scales, gout, va
 
         exp_bias = keep.tile([P, 1], F32, name="exp_bias")
         half_steep = keep.tile([P, 1], F32, name="half_steep")
-        nc.gpsimd.tensor_scalar(out=exp_bias[:], in0=lse_sb, scalar1=-1.0, scalar2=math.log(1024.0), op0=ALU.mult, op1=ALU.add)
         nc.gpsimd.tensor_scalar(out=half_steep[:], in0=steep_sb, scalar1=0.5, scalar2=0.0, op0=ALU.mult, op1=ALU.add)
+        nc.gpsimd.tensor_scalar(out=exp_bias[:], in0=lse_sb, scalar1=-1.0, scalar2=math.log(1024.0), op0=ALU.mult, op1=ALU.add)
 
         a_sb = keep.tile([P, T], F32, name="a_sb")
         for h in range(T // A_WIDTH):
@@ -110,11 +116,9 @@ def tile_attend_gboost_heads_kernel(tc, query, keys_words, keys_scales, gout, va
             a_ps = psum.tile([P, A_WIDTH], F32, name=f"a_ps{h}", tag=f"bank{h}")
             nc.tensor.matmul_mx(
                 out=a_ps[:], lhsT=q_codes[:].bitcast(FP8X4), lhsT_scale=q_scales[:],
-                rhs=k_codes[:, cols].bitcast(FP8X4), rhs_scale=k_scales[4 * h : P, :], start=True, stop=True,
+                rhs=k_codes[h // 2][:, (h % 2) * A_WIDTH : (h % 2 + 1) * A_WIDTH].bitcast(FP8X4), rhs_scale=k_scales[4 * h : P, :], start=True, stop=True,
             )
             nc.vector.tensor_copy(out=a_sb[:, cols], in_=a_ps[:])
-        interleave(nc, "vector", g_grp[:], g_raw[:])
-        g_codes, g_scales = quantize(nc, keep, "g", g_grp[:], Q)
         a_picked = keep.tile([P, SLOTS], F32, name="a_picked")
         nc.vector.tensor_copy(a_picked[:], a_sb[:].indirect(offsets[:]))
 
@@ -123,49 +127,49 @@ def tile_attend_gboost_heads_kernel(tc, query, keys_words, keys_scales, gout, va
 
         def quantize_load(n):
             first, width, on_vector = LOADS[n]
-            parts = []
-            for engine, lo, hi in (("vector", 0, on_vector), ("scalar", on_vector, width)):
-                if hi > lo:
-                    grp = keep.tile([P, hi - lo, PACK], BF16, name=f"v_grp{n}_{engine}", tag=f"v_grp{n}_{engine}", align_bytes=64)
-                    interleave(nc, engine, grp[:], v_raw[n][:, :, lo:hi])
-                    parts.append((grp, lo, hi))
-            v_codes = keep.tile([P, width], U32, name=f"v_codes{n}", align_bytes=64)
-            v_scales = keep.tile([P, width], U8, name=f"v_scales{n}", align_bytes=64)
-            for grp, lo, hi in reversed(parts):
-                nc.vector.quantize_mx(
-                    out=v_codes[:, lo:hi].bitcast(FP8X4), scales=v_scales[:, lo:hi], in_=grp[:].rearrange("p w t -> p (w t)")
-                )
-            return v_codes, v_scales
+            grp = keep.tile([P, width, PACK], BF16, name=f"v_grp{n}", tag=f"v_grp{n}", align_bytes=64)
+            interleave(nc, "scalar", grp[:, on_vector:width, :], v_raw[n][:, :, on_vector:width])
+            if on_vector > 0:
+                interleave(nc, "vector", grp[:, 0:on_vector, :], v_raw[n][:, :, 0:on_vector])
+            return quantize(nc, keep, f"v{n}", grp[:], width)
 
-        def multiply(dp, operand):
+        def multiply(n, operand):
             v_codes, v_scales = operand
+            dp = psum.tile([P, LOADS[n][1]], F32, name=f"dp{n}")
             nc.tensor.matmul_mx(
-                out=dp, lhsT=g_codes[:].bitcast(FP8X4), lhsT_scale=g_scales[:],
+                out=dp[:], lhsT=g_codes[:].bitcast(FP8X4), lhsT_scale=g_scales[:],
                 rhs=v_codes[:].bitcast(FP8X4), rhs_scale=v_scales[:], start=True, stop=True,
             )
+            return dp
 
-        def gradient(dp, first, width, tag):
-            cols = slice(first, first + width)
-            weight = keep.tile([P, width], F32, name=f"weight{first}", tag=tag)
-            nc.scalar.activation(out=weight[:], in_=a_sb[:, cols], func=ACT.Exp, bias=exp_bias[:])
+        def weights(first, width, n):
+            weight = reused[n][:, 0:width]
+            nc.scalar.activation(out=weight, in_=a_sb[:, first : first + width], func=ACT.Exp, bias=exp_bias[:])
+            return weight
+
+        def gradient(dp, weight, first):
             nc.vector.scalar_tensor_tensor(
-                out=ds[:, cols], in0=dp[:], scalar=delta_sb, in1=weight[:], op0=ALU.subtract, op1=ALU.mult
+                out=ds[:, first : first + 256], in0=dp[:], scalar=delta_sb, in1=weight, op0=ALU.subtract, op1=ALU.mult
             )
 
-        last = len(LOADS) - 1
-        products = []
-        for n, (first, width, on_vector) in enumerate(LOADS):
-            dp = psum.tile([P, width], F32, name=f"dp{n}")
-            multiply(dp[:], quantize_load(n))
-            products.append(dp)
-            if n == 1:
-                nc.scalar.activation(out=th[:], in_=a_picked[:], func=ACT.Tanh, scale=half_steep[:])
-            if n > 0:
-                gradient(products[n - 1], LOADS[n - 1][0], LOADS[n - 1][1], f"v_raw{n}")
-        gradient(products[last], LOADS[last][0], LOADS[last][1], "weight_last")
+        first_operand = quantize_load(0)
+        interleave(nc, "scalar", g_grp[:], g_raw[:])
+        g_codes, g_scales = quantize(nc, keep, "g", g_grp[:], Q)
+        nc.scalar.activation(out=th[:], in_=a_picked[:], func=ACT.Tanh, scale=half_steep[:])
+        dp0 = multiply(0, first_operand)
+        dp1 = multiply(1, quantize_load(1))
+        gradient(dp0, weights(0, 256, 1), 0)
+        dp2 = multiply(2, quantize_load(2))
+        gradient(dp1, weights(256, 256, 2), 256)
+        dp3 = multiply(3, quantize_load(3))
+        tail = weights(512, 512, 3)
+        gradient(dp2, tail[:, 0:256], 512)
+        gradient(dp3, tail[:, 256:512], 768)
 
-        gate = keep.tile([P, SLOTS], F32, name="gate", tag=f"v_grp{last}_scalar", align_bytes=64)
-        nc.scalar.activation(out=gate[:], in_=th[:], func=ACT.Copy, scale=0.5, bias=0.5)
+        gate = keep.tile([P, SLOTS], F32, name="gate", tag="v_grp3", align_bytes=64)
+        for h in range(2):
+            cols = slice(h * 256, (h + 1) * 256)
+            nc.scalar.activation(out=gate[:, cols], in_=th[:, cols], func=ACT.Copy, scale=0.5, bias=0.5)
 
         halves = 2
         width = SLOTS // halves

@@ -18,30 +18,27 @@ ACT = mybir.ActivationFunctionType
 
 P = 128
 PACK = 4
-BANK = 512
-A_WIDTH = 256
-
-LOADS = (
-    (0, 256, 0),
-    (256, 256, 192),
-    (512, 256, 160),
-    (768, 256, 160),
-)
+QUADRANT = 32
+STRETCH = 256
+STRETCHES = T // STRETCH
+KEY_LOAD = 512
+HALF = SLOTS // 2
+ON_VECTOR = (0, 144, 144, 144)
 
 
-def interleave(nc, engine, grouped, raw):
-    out = grouped.rearrange("p (c i) t -> p c t i", i=4)
-    src = raw.rearrange("p t (c i) -> p c t i", i=4)
-    if engine == "vector":
+def interleave(nc, on_vector, grouped, raw):
+    out = grouped.rearrange("p (c i) r -> p c r i", i=4)
+    src = raw.rearrange("p r (c i) -> p c r i", i=4)
+    if on_vector:
         nc.vector.tensor_copy(out=out, in_=src)
     else:
-        nc.scalar.copy(out=out, in_=src)
+        nc.scalar.activation(out=out, in_=src, func=ACT.Copy)
 
 
 def quantize(nc, pool, name, grouped, width):
     codes = pool.tile([P, width], U32, name=name + "_codes", align_bytes=64)
     scales = pool.tile([P, width], U8, name=name + "_scales", align_bytes=64)
-    nc.vector.quantize_mx(out=codes[:].bitcast(FP8X4), scales=scales[:], in_=grouped.rearrange("p w t -> p (w t)"))
+    nc.vector.quantize_mx(out=codes[:].bitcast(FP8X4), scales=scales[:], in_=grouped.rearrange("p c r -> p (c r)"))
     return codes, scales
 
 
@@ -54,133 +51,140 @@ def tile_attend_gboost_heads_kernel(tc, query, keys_words, keys_scales, gout, va
         offsets = keep.tile([P, SLOTS // 16], U16, name="offsets")
         q_raw = keep.tile([P, PACK, Q], F32, name="q_raw")
         g_raw = keep.tile([P, PACK, Q], F32, name="g_raw")
-        k_scales = keep.tile([P, A_WIDTH], U8, name="k_scales", align_bytes=64)
-        lse_t = keep.tile([P, 1], F32, name="lse_t")
-        steep_t = keep.tile([P, 1], F32, name="steep_t")
-        delta_t = keep.tile([P, 1], F32, name="delta_t")
-        lse_sb, steep_sb, delta_sb = lse_t[:], steep_t[:], delta_t[:]
-        warm_out = keep.tile([P, 1], F32, name="warm_out")
+        k_scales = keep.tile([P, STRETCH], U8, name="k_scales", align_bytes=64)
+        lse_sb = keep.tile([P, 1], F32, name="lse_sb")
+        steep_sb = keep.tile([P, 1], F32, name="steep_sb")
+        delta_sb = keep.tile([P, 1], F32, name="delta_sb")
         old_sb = keep.tile([P, SLOTS], F32, name="old_sb")
 
-        warm_in = keep.tile([P, 1], F32, name="warm_in")
-        nc.vector.memset(warm_in[:], 0.0)
-        nc.scalar.activation(out=warm_out[:], in_=warm_in[:], func=ACT.Exp)
-
-        v_rows = vals.rearrange("(p j) w -> p j w", j=PACK)
+        v_rows = vals.rearrange("(p r) t -> p r t", r=PACK)
         v_raw = []
-        reused = []
+        weight_room = []
 
         def load_vals(n):
-            first, width, on_vector = LOADS[n]
-            landing = keep.tile([P, PACK * width + 512], F32, name=f"landing{n}")
-            raw = landing[:, 0 : PACK * width].rearrange("p (j w) -> p j w", j=PACK)
-            nc.sync.dma_start(out=raw, in_=v_rows[:, :, first : first + width])
+            landing = keep.tile([P, (PACK + 2) * STRETCH], F32, name=f"landing{n}")
+            raw = landing[:, 0 : PACK * STRETCH].rearrange("p (r t) -> p r t", r=PACK)
+            nc.sync.dma_start(out=raw, in_=v_rows[:, :, n * STRETCH : (n + 1) * STRETCH])
             v_raw.append(raw)
-            reused.append(landing[:, (PACK - 1) * width + on_vector : PACK * width + 512])
+            weight_room.append(landing[:, (PACK - 1) * STRETCH + ON_VECTOR[n] : (PACK + 2) * STRETCH])
 
-        nc.sync.dma_start(out=q_raw[:], in_=query.rearrange("(p j) w -> p j w", j=PACK))
-        for quad in range(4):
+        nc.sync.dma_start(out=q_raw[:], in_=query.rearrange("(p r) q -> p r q", r=PACK))
+        for u in range(P // QUADRANT):
             nc.sync.dma_start(
-                out=k_scales[32 * quad : 32 * quad + 16, :].bitcast(I32),
-                in_=keys_scales[0, 4 * quad : 4 * quad + 4, :].bitcast(I32).rearrange("f (h c) -> h f c", h=T // A_WIDTH),
+                out=k_scales[QUADRANT * u : QUADRANT * u + 4 * STRETCHES, :].bitcast(I32),
+                in_=keys_scales[0, 4 * u : 4 * u + 4, :].bitcast(I32).rearrange("f (h c) -> h f c", h=STRETCHES),
             )
-        k_words = keys_words[0].rearrange("p n t -> p (n t)").bitcast(I32)
+        k_words = keys_words[0].rearrange("p t r -> p (t r)").bitcast(I32)
         k_codes = []
-        for h in range(T // BANK):
-            half = keep.tile([P, BANK], U32, name=f"k_codes{h}", align_bytes=64)
-            nc.sync.dma_start(out=half[:].bitcast(I32), in_=k_words[:, h * BANK : (h + 1) * BANK])
-            k_codes.append(half)
+        for n in range(T // KEY_LOAD):
+            codes = keep.tile([P, KEY_LOAD], U32, name=f"k_codes{n}", align_bytes=64)
+            nc.sync.dma_start(out=codes[:].bitcast(I32), in_=k_words[:, n * KEY_LOAD : (n + 1) * KEY_LOAD])
+            k_codes.append(codes)
         load_vals(0)
         nc.sync.dma_start(offsets[:], offs)
-        nc.sync.dma_start(out=g_raw[:], in_=gout.rearrange("(p j) w -> p j w", j=PACK))
-        nc.sync.dma_start(out=steep_sb, in_=steep)
-        nc.sync.dma_start(out=lse_sb, in_=lse)
-        nc.sync.dma_start(out=delta_sb, in_=delta)
-        for n in range(1, len(LOADS)):
+        nc.sync.dma_start(out=g_raw[:], in_=gout.rearrange("(p r) q -> p r q", r=PACK))
+        nc.sync.dma_start(out=steep_sb[:], in_=steep)
+        nc.sync.dma_start(out=lse_sb[:], in_=lse)
+        nc.sync.dma_start(out=delta_sb[:], in_=delta)
+        for n in range(1, STRETCHES):
             load_vals(n)
         nc.sync.dma_start(out=old_sb[:], in_=old)
 
         q_grp = keep.tile([P, Q, PACK], BF16, name="q_grp", align_bytes=64)
         g_grp = keep.tile([P, Q, PACK], BF16, name="g_grp", align_bytes=64)
-        interleave(nc, "vector", q_grp[:], q_raw[:])
+        interleave(nc, True, q_grp[:], q_raw[:])
         q_codes, q_scales = quantize(nc, keep, "q", q_grp[:], Q)
 
         exp_bias = keep.tile([P, 1], F32, name="exp_bias")
         half_steep = keep.tile([P, 1], F32, name="half_steep")
-        nc.gpsimd.tensor_scalar(out=half_steep[:], in0=steep_sb, scalar1=0.5, scalar2=0.0, op0=ALU.mult, op1=ALU.add)
-        nc.gpsimd.tensor_scalar(out=exp_bias[:], in0=lse_sb, scalar1=-1.0, scalar2=math.log(1024.0), op0=ALU.mult, op1=ALU.add)
+        nc.gpsimd.tensor_scalar(out=half_steep[:], in0=steep_sb[:], scalar1=0.5, scalar2=0.0, op0=ALU.mult, op1=ALU.add)
+        nc.gpsimd.tensor_scalar(
+            out=exp_bias[:], in0=lse_sb[:], scalar1=-1.0, scalar2=math.log(1024.0), op0=ALU.mult, op1=ALU.add
+        )
 
         a_sb = keep.tile([P, T], F32, name="a_sb")
-        for h in range(T // A_WIDTH):
-            cols = slice(h * A_WIDTH, (h + 1) * A_WIDTH)
-            a_ps = psum.tile([P, A_WIDTH], F32, name=f"a_ps{h}", tag=f"bank{h}")
+        for h in range(STRETCHES):
+            load, at = divmod(h * STRETCH, KEY_LOAD)
+            a_ps = psum.tile([P, STRETCH], F32, name=f"a_ps{h}")
             nc.tensor.matmul_mx(
-                out=a_ps[:], lhsT=q_codes[:].bitcast(FP8X4), lhsT_scale=q_scales[:],
-                rhs=k_codes[h // 2][:, (h % 2) * A_WIDTH : (h % 2 + 1) * A_WIDTH].bitcast(FP8X4), rhs_scale=k_scales[4 * h : P, :], start=True, stop=True,
+                out=a_ps[:],
+                lhsT=q_codes[:].bitcast(FP8X4),
+                lhsT_scale=q_scales[:],
+                rhs=k_codes[load][:, at : at + STRETCH].bitcast(FP8X4),
+                rhs_scale=k_scales[4 * h : P, :],
+                start=True,
+                stop=True,
             )
-            nc.vector.tensor_copy(out=a_sb[:, cols], in_=a_ps[:])
+            nc.vector.tensor_copy(out=a_sb[:, h * STRETCH : (h + 1) * STRETCH], in_=a_ps[:])
         a_picked = keep.tile([P, SLOTS], F32, name="a_picked")
         nc.vector.tensor_copy(a_picked[:], a_sb[:].indirect(offsets[:]))
 
         ds = keep.tile([P, T], F32, name="ds")
-        th = keep.tile([P, SLOTS], F32, name="th")
+        tanh_picked = keep.tile([P, SLOTS], F32, name="tanh_picked")
 
-        def quantize_load(n):
-            first, width, on_vector = LOADS[n]
-            grp = keep.tile([P, width, PACK], BF16, name=f"v_grp{n}", tag=f"v_grp{n}", align_bytes=64)
-            interleave(nc, "scalar", grp[:, on_vector:width, :], v_raw[n][:, :, on_vector:width])
-            if on_vector > 0:
-                interleave(nc, "vector", grp[:, 0:on_vector, :], v_raw[n][:, :, 0:on_vector])
-            return quantize(nc, keep, f"v{n}", grp[:], width)
+        def quantize_vals(n):
+            split = ON_VECTOR[n]
+            grp = keep.tile([P, STRETCH, PACK], BF16, name=f"v_grp{n}", tag=f"v_grp{n}", align_bytes=64)
+            interleave(nc, False, grp[:, split:STRETCH, :], v_raw[n][:, :, split:STRETCH])
+            if split > 0:
+                interleave(nc, True, grp[:, 0:split, :], v_raw[n][:, :, 0:split])
+            return quantize(nc, keep, f"v{n}", grp[:], STRETCH)
 
-        def multiply(n, operand):
-            v_codes, v_scales = operand
-            dp = psum.tile([P, LOADS[n][1]], F32, name=f"dp{n}")
+        def multiply(n, v_codes, v_scales):
+            dp = psum.tile([P, STRETCH], F32, name=f"dp{n}")
             nc.tensor.matmul_mx(
-                out=dp[:], lhsT=g_codes[:].bitcast(FP8X4), lhsT_scale=g_scales[:],
-                rhs=v_codes[:].bitcast(FP8X4), rhs_scale=v_scales[:], start=True, stop=True,
+                out=dp[:],
+                lhsT=g_codes[:].bitcast(FP8X4),
+                lhsT_scale=g_scales[:],
+                rhs=v_codes[:].bitcast(FP8X4),
+                rhs_scale=v_scales[:],
+                start=True,
+                stop=True,
             )
             return dp
 
-        def weights(first, width, n):
-            weight = reused[n][:, 0:width]
-            nc.scalar.activation(out=weight, in_=a_sb[:, first : first + width], func=ACT.Exp, bias=exp_bias[:])
+        def weights(first, count, room):
+            weight = room[:, 0 : count * STRETCH]
+            cols = slice(first * STRETCH, (first + count) * STRETCH)
+            nc.scalar.activation(out=weight, in_=a_sb[:, cols], func=ACT.Exp, bias=exp_bias[:])
             return weight
 
-        def gradient(dp, weight, first):
+        def gradient(n, dp, weight):
             nc.vector.scalar_tensor_tensor(
-                out=ds[:, first : first + 256], in0=dp[:], scalar=delta_sb, in1=weight, op0=ALU.subtract, op1=ALU.mult
+                out=ds[:, n * STRETCH : (n + 1) * STRETCH],
+                in0=dp[:],
+                scalar=delta_sb[:],
+                in1=weight,
+                op0=ALU.subtract,
+                op1=ALU.mult,
             )
 
-        first_operand = quantize_load(0)
-        interleave(nc, "scalar", g_grp[:], g_raw[:])
+        first_operand = quantize_vals(0)
+        interleave(nc, False, g_grp[:], g_raw[:])
         g_codes, g_scales = quantize(nc, keep, "g", g_grp[:], Q)
-        nc.scalar.activation(out=th[:], in_=a_picked[:], func=ACT.Tanh, scale=half_steep[:])
-        dp0 = multiply(0, first_operand)
-        dp1 = multiply(1, quantize_load(1))
-        gradient(dp0, weights(0, 256, 1), 0)
-        dp2 = multiply(2, quantize_load(2))
-        gradient(dp1, weights(256, 256, 2), 256)
-        dp3 = multiply(3, quantize_load(3))
-        tail = weights(512, 512, 3)
-        gradient(dp2, tail[:, 0:256], 512)
-        gradient(dp3, tail[:, 256:512], 768)
+        nc.scalar.activation(out=tanh_picked[:], in_=a_picked[:], func=ACT.Tanh, scale=half_steep[:])
 
-        gate = keep.tile([P, SLOTS], F32, name="gate", tag="v_grp3", align_bytes=64)
-        for h in range(2):
-            cols = slice(h * 256, (h + 1) * 256)
-            nc.scalar.activation(out=gate[:, cols], in_=th[:, cols], func=ACT.Copy, scale=0.5, bias=0.5)
+        last = STRETCHES - 1
+        previous = multiply(0, *first_operand)
+        for n in range(1, last):
+            dp = multiply(n, *quantize_vals(n))
+            gradient(n - 1, previous, weights(n - 1, 1, weight_room[n]))
+            previous = dp
+        dp = multiply(last, *quantize_vals(last))
+        last_weights = weights(last - 1, 2, weight_room[last])
+        gradient(last - 1, previous, last_weights[:, 0:STRETCH])
+        gradient(last, dp, last_weights[:, STRETCH : 2 * STRETCH])
 
-        halves = 2
-        width = SLOTS // halves
+        halves = [slice(h * HALF, (h + 1) * HALF) for h in range(SLOTS // HALF)]
+        gate = keep.tile([P, SLOTS], F32, name="gate", tag=f"v_grp{last}", align_bytes=64)
+        for cols in halves:
+            nc.scalar.activation(out=gate[:, cols], in_=tanh_picked[:, cols], func=ACT.Copy, scale=0.5, bias=0.5)
+
         gated = keep.tile([P, SLOTS], F32, name="gated")
-        for h in range(halves):
-            cols = slice(h * width, (h + 1) * width)
-            nc.vector.tensor_tensor(
-                gated[:, cols], ds[:].indirect(offsets[:, h * width // 16 : (h + 1) * width // 16]), gate[:, cols], ALU.mult
-            )
-        for h in range(halves):
-            cols = slice(h * width, (h + 1) * width)
-            res = keep.tile([P, width], F32, name=f"res{h}")
-            nc.vector.tensor_tensor(res[:], gated[:, cols], old_sb[:, cols], ALU.add)
-            nc.sync.dma_start(out=out[:, cols], in_=res[:])
+        for cols in halves:
+            picked = ds[:].indirect(offsets[:, cols.start // 16 : cols.stop // 16])
+            nc.vector.tensor_tensor(gated[:, cols], picked, gate[:, cols], ALU.mult)
+        for h, cols in enumerate(halves):
+            result = keep.tile([P, HALF], F32, name=f"result{h}")
+            nc.vector.tensor_tensor(result[:], gated[:, cols], old_sb[:, cols], ALU.add)
+            nc.sync.dma_start(out=out[:, cols], in_=result[:])

import math
from contextlib import ExitStack

import concourse.mybir as mybir

D, E, T, Q, SLOTS = 512, 512, 1024, 128, 512
FLOPS = 2 * Q * T * (D + E)

F32 = mybir.dt.float32
BF16 = mybir.dt.bfloat16
I32 = mybir.dt.int32
U32 = mybir.dt.uint32
U16 = mybir.dt.uint16
U8 = mybir.dt.uint8
FP8X4 = mybir.dt.float8_e4m3fn_x4
ALU = mybir.AluOpType
ACT = mybir.ActivationFunctionType

P = 128
PACK = 4
QUADRANT = 32
STRETCH = 256
STRETCHES = T // STRETCH
KEY_LOAD = 512
HALF = SLOTS // 2
ON_VECTOR = (0, 144, 144, 144)


def interleave(nc, on_vector, grouped, raw):
    out = grouped.rearrange("p (c i) r -> p c r i", i=4)
    src = raw.rearrange("p r (c i) -> p c r i", i=4)
    if on_vector:
        nc.vector.tensor_copy(out=out, in_=src)
    else:
        nc.scalar.activation(out=out, in_=src, func=ACT.Copy)


def quantize(nc, pool, name, grouped, width):
    codes = pool.tile([P, width], U32, name=name + "_codes", align_bytes=64)
    scales = pool.tile([P, width], U8, name=name + "_scales", align_bytes=64)
    nc.vector.quantize_mx(out=codes[:].bitcast(FP8X4), scales=scales[:], in_=grouped.rearrange("p c r -> p (c r)"))
    return codes, scales


def tile_attend_gboost_heads_kernel(tc, query, keys_words, keys_scales, gout, vals, lse, delta, steep, old, offs, out):
    nc = tc.nc
    with ExitStack() as ctx:
        keep = ctx.enter_context(tc.tile_pool(name="keep", bufs=1))
        psum = ctx.enter_context(tc.psum_pool(name="psum", bufs=1))

        offsets = keep.tile([P, SLOTS // 16], U16, name="offsets")
        q_raw = keep.tile([P, PACK, Q], F32, name="q_raw")
        g_raw = keep.tile([P, PACK, Q], F32, name="g_raw")
        k_scales = keep.tile([P, STRETCH], U8, name="k_scales", align_bytes=64)
        lse_sb = keep.tile([P, 1], F32, name="lse_sb")
        steep_sb = keep.tile([P, 1], F32, name="steep_sb")
        delta_sb = keep.tile([P, 1], F32, name="delta_sb")
        old_sb = keep.tile([P, SLOTS], F32, name="old_sb")

        v_rows = vals.rearrange("(p r) t -> p r t", r=PACK)
        v_raw = []
        weight_room = []

        def load_vals(n):
            landing = keep.tile([P, (PACK + 2) * STRETCH], F32, name=f"landing{n}")
            raw = landing[:, 0 : PACK * STRETCH].rearrange("p (r t) -> p r t", r=PACK)
            nc.sync.dma_start(out=raw, in_=v_rows[:, :, n * STRETCH : (n + 1) * STRETCH])
            v_raw.append(raw)
            weight_room.append(landing[:, (PACK - 1) * STRETCH + ON_VECTOR[n] : (PACK + 2) * STRETCH])

        nc.sync.dma_start(out=q_raw[:], in_=query.rearrange("(p r) q -> p r q", r=PACK))
        for u in range(P // QUADRANT):
            nc.sync.dma_start(
                out=k_scales[QUADRANT * u : QUADRANT * u + 4 * STRETCHES, :].bitcast(I32),
                in_=keys_scales[0, 4 * u : 4 * u + 4, :].bitcast(I32).rearrange("f (h c) -> h f c", h=STRETCHES),
            )
        k_words = keys_words[0].rearrange("p t r -> p (t r)").bitcast(I32)
        k_codes = []
        for n in range(T // KEY_LOAD):
            codes = keep.tile([P, KEY_LOAD], U32, name=f"k_codes{n}", align_bytes=64)
            nc.sync.dma_start(out=codes[:].bitcast(I32), in_=k_words[:, n * KEY_LOAD : (n + 1) * KEY_LOAD])
            k_codes.append(codes)
        load_vals(0)
        nc.sync.dma_start(offsets[:], offs)
        nc.sync.dma_start(out=g_raw[:], in_=gout.rearrange("(p r) q -> p r q", r=PACK))
        nc.sync.dma_start(out=steep_sb[:], in_=steep)
        nc.sync.dma_start(out=lse_sb[:], in_=lse)
        nc.sync.dma_start(out=delta_sb[:], in_=delta)
        for n in range(1, STRETCHES):
            load_vals(n)
        nc.sync.dma_start(out=old_sb[:], in_=old)

        q_grp = keep.tile([P, Q, PACK], BF16, name="q_grp", align_bytes=64)
        g_grp = keep.tile([P, Q, PACK], BF16, name="g_grp", align_bytes=64)
        interleave(nc, True, q_grp[:], q_raw[:])
        q_codes, q_scales = quantize(nc, keep, "q", q_grp[:], Q)

        exp_bias = keep.tile([P, 1], F32, name="exp_bias")
        half_steep = keep.tile([P, 1], F32, name="half_steep")
        nc.gpsimd.tensor_scalar(out=half_steep[:], in0=steep_sb[:], scalar1=0.5, scalar2=0.0, op0=ALU.mult, op1=ALU.add)
        nc.gpsimd.tensor_scalar(
            out=exp_bias[:], in0=lse_sb[:], scalar1=-1.0, scalar2=math.log(1024.0), op0=ALU.mult, op1=ALU.add
        )

        a_sb = keep.tile([P, T], F32, name="a_sb")
        for h in range(STRETCHES):
            load, at = divmod(h * STRETCH, KEY_LOAD)
            a_ps = psum.tile([P, STRETCH], F32, name=f"a_ps{h}")
            nc.tensor.matmul_mx(
                out=a_ps[:],
                lhsT=q_codes[:].bitcast(FP8X4),
                lhsT_scale=q_scales[:],
                rhs=k_codes[load][:, at : at + STRETCH].bitcast(FP8X4),
                rhs_scale=k_scales[4 * h : P, :],
                start=True,
                stop=True,
            )
            nc.vector.tensor_copy(out=a_sb[:, h * STRETCH : (h + 1) * STRETCH], in_=a_ps[:])
        a_picked = keep.tile([P, SLOTS], F32, name="a_picked")
        nc.vector.tensor_copy(a_picked[:], a_sb[:].indirect(offsets[:]))

        ds = keep.tile([P, T], F32, name="ds")
        tanh_picked = keep.tile([P, SLOTS], F32, name="tanh_picked")

        def quantize_vals(n):
            split = ON_VECTOR[n]
            grp = keep.tile([P, STRETCH, PACK], BF16, name=f"v_grp{n}", tag=f"v_grp{n}", align_bytes=64)
            interleave(nc, False, grp[:, split:STRETCH, :], v_raw[n][:, :, split:STRETCH])
            if split > 0:
                interleave(nc, True, grp[:, 0:split, :], v_raw[n][:, :, 0:split])
            return quantize(nc, keep, f"v{n}", grp[:], STRETCH)

        def multiply(n, v_codes, v_scales):
            dp = psum.tile([P, STRETCH], F32, name=f"dp{n}")
            nc.tensor.matmul_mx(
                out=dp[:],
                lhsT=g_codes[:].bitcast(FP8X4),
                lhsT_scale=g_scales[:],
                rhs=v_codes[:].bitcast(FP8X4),
                rhs_scale=v_scales[:],
                start=True,
                stop=True,
            )
            return dp

        def weights(first, count, room):
            weight = room[:, 0 : count * STRETCH]
            cols = slice(first * STRETCH, (first + count) * STRETCH)
            nc.scalar.activation(out=weight, in_=a_sb[:, cols], func=ACT.Exp, bias=exp_bias[:])
            return weight

        def gradient(n, dp, weight):
            nc.vector.scalar_tensor_tensor(
                out=ds[:, n * STRETCH : (n + 1) * STRETCH],
                in0=dp[:],
                scalar=delta_sb[:],
                in1=weight,
                op0=ALU.subtract,
                op1=ALU.mult,
            )

        first_operand = quantize_vals(0)
        interleave(nc, False, g_grp[:], g_raw[:])
        g_codes, g_scales = quantize(nc, keep, "g", g_grp[:], Q)
        nc.scalar.activation(out=tanh_picked[:], in_=a_picked[:], func=ACT.Tanh, scale=half_steep[:])

        last = STRETCHES - 1
        previous = multiply(0, *first_operand)
        for n in range(1, last):
            dp = multiply(n, *quantize_vals(n))
            gradient(n - 1, previous, weights(n - 1, 1, weight_room[n]))
            previous = dp
        dp = multiply(last, *quantize_vals(last))
        last_weights = weights(last - 1, 2, weight_room[last])
        gradient(last - 1, previous, last_weights[:, 0:STRETCH])
        gradient(last, dp, last_weights[:, STRETCH : 2 * STRETCH])

        halves = [slice(h * HALF, (h + 1) * HALF) for h in range(SLOTS // HALF)]
        gate = keep.tile([P, SLOTS], F32, name="gate", tag=f"v_grp{last}", align_bytes=64)
        for cols in halves:
            nc.scalar.activation(out=gate[:, cols], in_=tanh_picked[:, cols], func=ACT.Copy, scale=0.5, bias=0.5)

        gated = keep.tile([P, SLOTS], F32, name="gated")
        for cols in halves:
            picked = ds[:].indirect(offsets[:, cols.start // 16 : cols.stop // 16])
            nc.vector.tensor_tensor(gated[:, cols], picked, gate[:, cols], ALU.mult)
        for h, cols in enumerate(halves):
            result = keep.tile([P, HALF], F32, name=f"result{h}")
            nc.vector.tensor_tensor(result[:], gated[:, cols], old_sb[:, cols], ALU.add)
            nc.sync.dma_start(out=out[:, cols], in_=result[:])
